import numpy as np, ml_dtypes
CORES = [78,86,94,102,110,118]
N = 6
import mx_ref
NC, KT, G, ROOT = 128, 2, 4, 1
C = np.float32(0.023)
BF = ml_dtypes.bfloat16
def cut(t, i, w=512):
    return t[:, w * i:w * i + w]
def tile(rs):
    return np.stack(rs, axis=2).reshape(128, -1).astype(BF)
def layer(w, X):
    out = []
    for i in range(G):
        for t in range(len(X)):
            p = mx_ref.matmul(mx_ref.quantize(cut(w, len(X) * i + t)), X[t])
            z = p if t == 0 else z + p
        out.append(z)
    return out
def act(Z):
    return [np.maximum(z, 0) * C for z in Z]
def setup_inputs(rng):
    def f(*shape):
        return mx_ref.flush((rng.standard_normal(shape, dtype=np.float32) * np.exp2(rng.integers(-2, 3, shape[:-1] + (1,)))).astype(BF))
    return {"x": f(N, 128, KT * 4 * NC), "w1": f(N, 128, G * KT * 512), "w2": f(N, 128, 512)}
def setup_inputs_blocks(rng):
    d = setup_inputs(rng)
    for k in ("x", "w1", "w2"): d[k] = mx_ref.spread(d[k], rng, 4)
    return d
def setup_inputs_wide(rng):
    d = setup_inputs(rng)
    for k in ("x", "w1", "w2"): d[k] = mx_ref.flush((d[k].astype(np.float32) * np.exp2(rng.integers(-8, 9, (N, 1, 1))).astype(np.float32)).astype(BF))
    return d
def setup_inputs_zeros(rng):
    d = setup_inputs(rng); v = d["x"].reshape(N, 128, -1, 4).copy()
    v[np.broadcast_to((rng.random((N, 1, v.shape[2], 1)) < 0.33), v.shape)] = 0
    d["x"] = v.reshape(d["x"].shape)
    return d
def reference(x, w1, w2):
    h = mx_ref.quantize(tile(act(layer(w1[ROOT], [mx_ref.quantize(cut(x[ROOT], t, 4 * NC)) for t in range(KT)]))))
    y = np.zeros((N, 128, NC), np.float32)
    for r in range(N):
        y[r] = mx_ref.matmul(mx_ref.quantize(w2[r]), h)
    return {"y": y}

from concourse.bass import DstId, RemoteDMATransfer
from concourse.mybir import dt, ActivationFunctionType

NC = 128
TW = 4 * NC
KT, G = 2, 4
FACTOR = 0.023
HEAD = 3

SCRATCH = {
    "xb": ("sbuf", [128, KT * TW], "bfloat16"),
    "xq": ("sbuf", [128, KT * NC], "float8_e4m3fn_x4"),
    "xs": ("sbuf", [128, KT * NC], "uint8"),
    "w1b": ("sbuf", [128, G * KT * TW], "bfloat16"),
    "w1q": ("sbuf", [128, G * KT * NC], "float8_e4m3fn_x4"),
    "w1s": ("sbuf", [128, G * KT * NC], "uint8"),
    "w2b": ("sbuf", [128, TW], "bfloat16"),
    "w2q": ("sbuf", [128, NC], "float8_e4m3fn_x4"),
    "w2s": ("sbuf", [128, NC], "uint8"),
    "z": ("psum", [128, 512 * G], "float32"),
    "hb": ("sbuf", [128, TW], "bfloat16"),
    "hq": ("sbuf", [128, NC], "float8_e4m3fn_x4"),
    "hs": ("sbuf", [128, NC], "uint8"),
    "yp": ("psum", [128, 512], "float32"),
    "yb": ("sbuf", [128, NC], "float32"),
}
SEMAPHORES = ["ldx", "ldhead", "ldtail", "ldw", "qx", "qw", "qh", "acts", "ymm", "ycp", "sent", "arrc", "arrp",
              "stored", "qt0", "qt1", "qt2", "qt3", "qt4", "qt5", "qt6", "qt7", "z0", "z1", "z2", "z3"]


def routes(T, topo):
    root = T.cores[T.root]
    return {root: [[c for c in T.cores if c != root]]}


def send(g, core, T, topo, dsts, view, sem):
    mask = None
    for d in dsts:
        if not topo.may_write(core, d):
            raise ValueError("core %d may not write to core %d" % (core, d))
        mask = topo.mask(core, d) if mask is None else mask & topo.mask(core, d)
    ids = [DstId(rid=topo.addr(d)[0], pnc=topo.addr(d)[1]) for d in dsts]
    g.remote_dma_fused([RemoteDMATransfer(dst_ids=ids, dma_engine_mask=mask, remote_sem=sem,
                                          srcs=[view], dsts=[view for _ in dsts])], local_sem=T.sem.sent)
    return bin(mask).count("1")


def first_layer(g, T):
    S = T.sem
    cut = HEAD * KT * TW
    g.sync.dma_start(out=T.xb[:], in_=T.x[:]).then_inc(S.ldx, 16)
    g.scalar.dma_start(out=T.w1b[:, 0:cut], in_=T.w1[:, 0:cut]).then_inc(S.ldhead, 16)
    g.sync.dma_start(out=T.w1b[:, cut:], in_=T.w1[:, cut:]).then_inc(S.ldtail, 16)

    g.vector.wait_ge(S.ldx, 16)
    g.vector.quantize_mx(out=T.xq[:], scales=T.xs[:], in_=T.xb[:]).then_inc(S.qx, 1)
    g.vector.wait_ge(S.ldhead, 16)
    for i in range(HEAD):
        a, b = KT * i * NC, KT * (i + 1) * NC
        g.vector.quantize_mx(out=T.w1q[:, a:b], scales=T.w1s[:, a:b],
                             in_=T.w1b[:, 4 * a:4 * b]).then_inc(S["qt%d" % (KT * i)], 1)
    g.vector.wait_ge(S.ldtail, 16)
    for k in range(HEAD * KT, G * KT):
        a, b = k * NC, (k + 1) * NC
        g.vector.quantize_mx(out=T.w1q[:, a:b], scales=T.w1s[:, a:b],
                             in_=T.w1b[:, 4 * a:4 * b]).then_inc(S["qt%d" % k], 1)

    g.tensor.wait_ge(S.qx, 1)
    for i in range(G):
        for t in range(KT):
            k = KT * i + t
            if i >= HEAD or t == 0:
                g.tensor.wait_ge(S["qt%d" % k], 1)
            mm = g.tensor.matmul_mx(out=T.z[:, 512 * i:512 * i + NC],
                                    lhsT=T.w1q[:, k * NC:(k + 1) * NC], lhsT_scale=T.w1s[:, k * NC:(k + 1) * NC],
                                    rhs=T.xq[:, t * NC:(t + 1) * NC], rhs_scale=T.xs[:, t * NC:(t + 1) * NC],
                                    start=(t == 0), stop=(t == KT - 1))
        mm.then_inc(S["z%d" % i], 1)

    for i in range(G):
        g.scalar.wait_ge(S["z%d" % i], 1)
        g.scalar.activation(out=T.hb[:, i:TW:G], in_=T.z[:, 512 * i:512 * i + NC],
                            func=ActivationFunctionType.Relu, scale=FACTOR).then_inc(S.acts, 1)

    g.vector.wait_ge(S.acts, G)
    g.vector.quantize_mx(out=T.hq[:], scales=T.hs[:], in_=T.hb[:]).then_inc(S.qh, 1)


def rank_program(g, core, T, topo):
    rank = T.rank_of(core)
    if rank is None:
        return
    S = T.sem
    is_root = rank == T.root
    groups = routes(T, topo).get(core, [])

    if is_root:
        first_layer(g, T)

    g.sync.dma_start(out=T.w2b[:], in_=T.w2[:]).then_inc(S.ldw, 16)
    g.vector.wait_ge(S.ldw, 16)
    g.vector.quantize_mx(out=T.w2q[:], scales=T.w2s[:], in_=T.w2b[:]).then_inc(S.qw, 1)

    left = 0
    if groups:
        if is_root:
            g.wait_ge(S.qh, 1)
        for dsts in groups:
            left += send(g, core, T, topo, dsts, T.hq[:].bitcast(dt.uint8), S.arrc)
            left += send(g, core, T, topo, dsts, T.hs[:], S.arrp)
        g.wait_ge(S.sent, left)

    g.tensor.wait_ge(S.qw, 1)
    if is_root:
        g.tensor.wait_ge(S.qh, 1)
    else:
        n = bin(topo.mask(T.cores[T.root], core)).count("1")
        g.tensor.wait_ge(S.arrc, n)
        g.tensor.wait_ge(S.arrp, n)
    g.tensor.matmul_mx(out=T.yp[:, 0:NC], lhsT=T.w2q[:], lhsT_scale=T.w2s[:], rhs=T.hq[:], rhs_scale=T.hs[:],
                       start=True, stop=True).then_inc(S.ymm, 1)
    g.vector.wait_ge(S.ymm, 1)
    g.vector.tensor_copy(out=T.yb[:], in_=T.yp[:, 0:NC]).then_inc(S.ycp, 1)
    g.sync.wait_ge(S.ycp, 1)
    if left:
        g.sync.wait_ge(S.sent, left)
    g.sync.dma_start(out=T.y[:], in_=T.yb[:]).then_inc(S.stored, 16)
    g.sync.wait_ge(S.stored, 16)
